import numpy as np
import ml_dtypes


def mxq(x, axis, fmt="e4m3"):
    dtype, down = {"e4m3": (ml_dtypes.float8_e4m3fn, 7), "e5m2": (ml_dtypes.float8_e5m2, 14)}[fmt]
    v = np.moveaxis(np.asarray(x, np.float32).astype(ml_dtypes.bfloat16).astype(np.float64), axis, -1)
    blocks = v.reshape(v.shape[:-1] + (-1, 32))
    amax = np.abs(blocks).max(-1, keepdims=True)
    byte = np.maximum(np.where(amax > 0, np.frexp(amax)[1] - 1 + 127, 0) - down, 1)
    scale = np.exp2(byte - 127.0)
    codes = (blocks / scale).astype(np.float32).astype(dtype).astype(np.float64)
    return np.moveaxis((codes * scale).reshape(v.shape), -1, axis)


WIDE = False


def mx_kscale(k):
    if not WIDE:
        return np.ones(k)
    levels = np.array([10, -10, 5, -5, 0])
    if k % 512:
        return np.exp2(np.random.permutation(np.resize(levels, k // 32))).repeat(32)
    a = np.empty((k // 512, 16))
    for p in range(k // 512):
        a[p, :8] = np.random.permutation(np.resize(levels, 8))
        for g in range(8):
            far = levels[np.abs(levels - a[p, g]) >= 10]
            a[p, g + 8] = far[np.random.randint(len(far))]
    return np.exp2(a.ravel()).repeat(32)


def f64(x):
    return np.asarray(x).astype(np.float64)


def striped(idx):
    return np.tile(np.asarray(idx).reshape(-1, 16).T, (8, 1)).astype(np.uint16)


def unstriped(offs):
    return offs[:16].T.reshape(-1).astype(np.int64)


E2M1 = np.array([0.0, 0.5, 1.0, 1.5, 2.0, 3.0, 4.0, 6.0, -0.0, -0.5, -1.0, -1.5, -2.0, -3.0, -4.0, -6.0])


def pack_weight(w, fmt):
    k, n = w.shape
    w = f64(np.asarray(w, np.float32).astype(ml_dtypes.bfloat16)).reshape(k // 32, 32, n)
    amax = np.abs(w).max(1)
    if fmt == "e4m3":
        byte = np.frexp(amax)[1] - 1 + 127 - 7
    else:
        mant, ex = np.frexp(amax / 6.0)
        byte = np.where(mant > 0.5, ex, ex - 1) + 127
    byte = np.clip(np.where(amax > 0, byte, 1), 1, 254)
    scaled = (w * np.exp2(127.0 - byte)[:, None, :]).reshape(k, n).astype(np.float32)
    by_word = np.ascontiguousarray(scaled.reshape(k // 512, 128, 4, n).transpose(0, 1, 3, 2))
    if fmt == "e4m3":
        words = by_word.astype(ml_dtypes.float8_e4m3fn).view(np.uint8)
    else:
        c = by_word.astype(ml_dtypes.float4_e2m1fn).view(np.uint8) & 0xF
        words = (c[..., 0::2] | (c[..., 1::2] << 4)).reshape(k // 512, 128, 2 * n)
    return np.ascontiguousarray(words), np.ascontiguousarray(byte.astype(np.uint8).reshape(k // 512, 16, n))


def unpack_weight(words, scales, fmt):
    g, _, n = scales.shape
    words = np.ascontiguousarray(words).reshape(g, 128, n, -1)
    if fmt == "e4m3":
        vals = words.view(ml_dtypes.float8_e4m3fn).astype(np.float64)
    else:
        nib = np.empty((g, 128, n, 4), np.uint8)
        nib[..., 0::2] = words & 0xF
        nib[..., 1::2] = words >> 4
        vals = E2M1[nib]
    vals = vals * np.repeat(np.exp2(scales.astype(np.float64) - 127.0), 8, axis=1)[..., None]
    return vals.transpose(0, 1, 3, 2).reshape(g * 512, n)


K, V, T, J, N = 512, 512, 1024, 512, 512


def setup_inputs():
    n = np.random.standard_normal
    idx = np.random.permutation(T)[:J]
    idx2 = np.random.randint(0, V, J)
    fk = mx_kscale(K)
    pqp = pack_weight(n((K, V)) / fk[:, None], "e2m1")
    wqp = pack_weight(n((K, N)) * 1 / np.sqrt(K) * fk[:, None], "e2m1")
    wfp = pack_weight(n((K, N)) * 1 / np.sqrt(K) * fk[:, None], "e4m3")
    return {
        "pq_words": pqp[0],
        "pq_scales": pqp[1],
        "wq_words": wqp[0],
        "wq_scales": wqp[1],
        "xf": (n((K, T)) / fk[:, None]).astype(np.float32),
        "pf": (n((K, V)) / fk[:, None]).astype(np.float32),
        "wf_words": wfp[0],
        "wf_scales": wfp[1],
        "offs": striped(idx),
        "offs2": striped(idx2),
    }


def reference(pq_words, pq_scales, wq_words, wq_scales, xf, pf, wf_words, wf_scales, offs, offs2):
    idx = unstriped(offs)
    idx2 = unstriped(offs2)
    pqu = unpack_weight(pq_words, pq_scales, "e2m1")
    wqu = unpack_weight(wq_words, wq_scales, "e2m1")
    wfu = unpack_weight(wf_words, wf_scales, "e4m3")
    z = wqu.T @ pqu
    d = f64(xf)[:, idx] - f64(pf)[:, idx2]
    dq = mxq(d, 0, "e4m3")
    p = wfu.T @ dq
    y = z[:, idx2] + np.tanh(p)
    return y

@@ -1,0 +1,156 @@
+from contextlib import ExitStack
+
+import concourse.mybir as mybir
+
+K, V, T, J, N = 512, 512, 1024, 512, 512
+FLOPS = 2 * K * N * V + 2 * K * N * J
+
+F32 = mybir.dt.float32
+BF16 = mybir.dt.bfloat16
+I32 = mybir.dt.int32
+U32 = mybir.dt.uint32
+U16 = mybir.dt.uint16
+U8 = mybir.dt.uint8
+FP8X4 = mybir.dt.float8_e4m3fn_x4
+FP4X4 = mybir.dt.float4_e2m1fn_x4
+ADD = mybir.AluOpType.add
+SUB = mybir.AluOpType.subtract
+TANH = mybir.ActivationFunctionType.Tanh
+
+P = 128
+PACK = 4
+HALF = J // 2
+LIST_COLS = HALF // 16
+M_TILES = N // P
+
+
+def load_scales(queue, plane, scales):
+    for q in range(4):
+        queue.dma_start(plane[32 * q : 32 * q + 4, :].bitcast(I32), scales[0, 4 * q : 4 * q + 4, :].bitcast(I32))
+
+
+def tile_list_remainder_on_prototype_kernel(tc, pq_words, pq_scales, wq_words, wq_scales, xf, pf, wf_words, wf_scales, offs, offs2, out):
+    nc = tc.nc
+    with ExitStack() as ctx:
+        lists = ctx.enter_context(tc.tile_pool(name="lists", bufs=1))
+        sb = ctx.enter_context(tc.tile_pool(name="sb", bufs=1))
+        psum = ctx.enter_context(tc.psum_pool(name="psum", bufs=8))
+
+        tok_list = lists.tile([P, J // 16], U16, name="tok_list")
+        proto_list = lists.tile([P, J // 16], U16, name="proto_list")
+        pf_rows = pf.rearrange("(p i) v -> p i v", i=PACK)
+        xf_rows = xf.rearrange("(p i) t -> p i t", i=PACK)
+
+        pf0 = sb.tile([P, V], F32, name="pf0")
+        pf1 = sb.tile([P, V], F32, name="pf1")
+        pf23 = sb.tile([P, 2, V], F32, name="pf23")
+        pf_planes = [pf0[:], pf1[:], pf23[:, 0, :], pf23[:, 1, :]]
+        xf_planes = [sb.tile([P, T], F32, name="xf%d" % i) for i in range(PACK)]
+        wq_codes = sb.tile([P, 2 * N], U8, name="wq_codes", align_bytes=64)
+        pq_codes = sb.tile([P, 2 * V], U8, name="pq_codes", align_bytes=64)
+        wf_codes = sb.tile([P, N], U32, name="wf_codes", align_bytes=64)
+        wq_plane = sb.tile([P, N], U8, name="wq_plane", align_bytes=64)
+        pq_plane = sb.tile([P, V], U8, name="pq_plane", align_bytes=64)
+        wf_plane = sb.tile([P, N], U8, name="wf_plane", align_bytes=64)
+
+        warm = sb.tile([P, 8], F32, name="warm")
+        warm_out = sb.tile([P, 8], F32, name="warm_out")
+        nc.vector.memset(warm[:], 0.0)
+
+        nc.sync.dma_start(proto_list[:], offs2)
+        nc.sync.dma_start(pf0[:], pf_rows[:, 0, :])
+        nc.sync.dma_start(pf1[:], pf_rows[:, 1, :])
+        nc.sync.dma_start(pf23[:], pf_rows[:, 2:4, :])
+        load_scales(nc.scalar, wq_plane, wq_scales)
+        nc.scalar.activation(warm_out[:], warm[:], TANH)
+        load_scales(nc.scalar, pq_plane, pq_scales)
+        nc.scalar.dma_start(wq_codes[:].bitcast(I32), wq_words[0].bitcast(I32))
+        nc.scalar.dma_start(pq_codes[:].bitcast(I32), pq_words[0].bitcast(I32))
+        for i in range(PACK):
+            if i == 2:
+                nc.sync.dma_start(tok_list[:], offs)
+            nc.sync.dma_start(xf_planes[i][:], xf_rows[:, i, :])
+        nc.sync.dma_start(wf_codes[:].bitcast(I32), wf_words[0].rearrange("p n t -> p (n t)").bitcast(I32))
+        load_scales(nc.sync, wf_plane, wf_scales)
+
+        def half_cols(h):
+            return slice(h * HALF, (h + 1) * HALF)
+
+        def list_half(tile, h):
+            return tile[:, h * LIST_COLS : (h + 1) * LIST_COLS]
+
+        picked = [sb.tile([P, PACK, HALF], F32, name="picked%d" % h, tag="stage%d" % h, align_bytes=64) for h in range(2)]
+        for i in range(PACK):
+            for h in range(2):
+                nc.vector.tensor_copy(picked[h][:, i, :], pf_planes[i].indirect(list_half(proto_list, h)))
+
+        z_tiles = [sb.tile([P, V], F32, name="z%d" % m) for m in range(M_TILES)]
+        for m in range(M_TILES):
+            bank = psum.tile([P, V], F32, name="bank")
+            nc.tensor.matmul_mx(
+                out=bank[:],
+                lhsT=wq_codes[:, 2 * P * m : 2 * P * (m + 1)].bitcast(FP4X4),
+                lhsT_scale=wq_plane[:, P * m : P * (m + 1)],
+                rhs=pq_codes[:].bitcast(FP4X4),
+                rhs_scale=pq_plane[:],
+                start=True,
+                stop=True,
+            )
+            nc.scalar.copy(z_tiles[m][:], bank[:])
+
+        d32 = {}
+        d16 = {}
+        d_codes = [sb.tile([P, HALF], U32, name="d_codes%d" % h, align_bytes=64) for h in range(2)]
+        d_plane = [sb.tile([P, HALF], U8, name="d_plane%d" % h, align_bytes=64) for h in range(2)]
+        act = [sb.tile([P, M_TILES, HALF], F32, name="act%d" % h) for h in range(2)]
+        res = [sb.tile([P, M_TILES, HALF], F32, name="res%d" % h) for h in range(2)]
+        out_rows = out.rearrange("(m p) j -> p m j", p=P)
+
+        def remainder(h):
+            d32[h] = sb.tile([P, PACK, HALF], F32, name="d32_%d" % h, tag=("stage2", "stage0")[h], align_bytes=64)
+            for i in range(PACK):
+                nc.vector.tensor_tensor(d32[h][:, i, :], xf_planes[i][:].indirect(list_half(tok_list, h)), picked[h][:, i, :], SUB)
+
+        def weave(h, copy):
+            d16[h] = sb.tile([P, HALF, PACK], BF16, name="d16_%d" % h, tag=("stage3", "stage2")[h], align_bytes=64)
+            copy(d16[h][:].rearrange("p (c e) i -> p c i e", e=4), d32[h][:].rearrange("p i (c e) -> p c i e", e=4))
+
+        def quantise(h):
+            nc.vector.quantize_mx(out=d_codes[h][:].bitcast(FP8X4), scales=d_plane[h][:], in_=d16[h][:].rearrange("p j i -> p (j i)"))
+
+        def product(h):
+            for m in range(M_TILES):
+                bank = psum.tile([P, V], F32, name="bank")
+                nc.tensor.matmul_mx(
+                    out=bank[:, 0:HALF],
+                    lhsT=wf_codes[:, P * m : P * (m + 1)].bitcast(FP8X4),
+                    lhsT_scale=wf_plane[:, P * m : P * (m + 1)],
+                    rhs=d_codes[h][:].bitcast(FP8X4),
+                    rhs_scale=d_plane[h][:],
+                    start=True,
+                    stop=True,
+                )
+                nc.scalar.activation(act[h][:, m, :], bank[:, 0:HALF], TANH)
+
+        def finish(h, m):
+            nc.vector.tensor_tensor(res[h][:, m, :], z_tiles[m][:].indirect(list_half(proto_list, h)), act[h][:, m, :], ADD)
+
+        def store(h, m0, m1):
+            nc.sync.dma_start(out_rows[:, m0:m1, half_cols(h)], res[h][:, m0:m1, :])
+
+        remainder(0)
+        weave(0, nc.scalar.copy)
+        quantise(0)
+        product(0)
+        remainder(1)
+        weave(1, nc.vector.tensor_copy)
+        finish(0, 0)
+        quantise(1)
+        product(1)
+        for m in range(1, M_TILES):
+            finish(0, m)
+        store(0, 0, 4)
+        for m in range(M_TILES):
+            finish(1, m)
+            if m > 0:
+                store(1, 0 if m == 1 else m, m + 1)

@@ -22,6 +22,8 @@ PACK = 4
 HALF = J // 2
 LIST_COLS = HALF // 16
 M_TILES = N // P
+CHUNKS = ((0, 256), (256, 512))
+WINDOW = 704
 
 
 def load_scales(queue, plane, scales):
@@ -41,10 +43,10 @@ def tile_list_remainder_on_prototype_kernel(tc, pq_words, pq_scales, wq_words, w
         pf_rows = pf.rearrange("(p i) v -> p i v", i=PACK)
         xf_rows = xf.rearrange("(p i) t -> p i t", i=PACK)
 
-        pf0 = sb.tile([P, V], F32, name="pf0")
-        pf1 = sb.tile([P, V], F32, name="pf1")
-        pf23 = sb.tile([P, 2, V], F32, name="pf23")
-        pf_planes = [pf0[:], pf1[:], pf23[:, 0, :], pf23[:, 1, :]]
+        pf0 = sb.tile([P, WINDOW], F32, name="pf0")
+        pf1 = sb.tile([P, WINDOW], F32, name="pf1")
+        pf23 = sb.tile([P, V + WINDOW], F32, name="pf23")
+        pf_planes = [pf0[:], pf1[:], pf23[:, 0:WINDOW], pf23[:, V:]]
         xf_planes = [sb.tile([P, T], F32, name="xf%d" % i) for i in range(PACK)]
         wq_codes = sb.tile([P, 2 * N], U8, name="wq_codes", align_bytes=64)
         pq_codes = sb.tile([P, 2 * V], U8, name="pq_codes", align_bytes=64)
@@ -56,16 +58,19 @@ def tile_list_remainder_on_prototype_kernel(tc, pq_words, pq_scales, wq_words, w
         warm = sb.tile([P, 8], F32, name="warm")
         warm_out = sb.tile([P, 8], F32, name="warm_out")
         nc.vector.memset(warm[:], 0.0)
+        nc.vector.memset(pf0[:, V:], 0.0)
+        nc.vector.memset(pf1[:, V:], 0.0)
+        nc.vector.memset(pf23[:, 2 * V :], 0.0)
 
+        nc.sync.dma_start(pf0[:, 0:V], pf_rows[:, 0, :])
         nc.sync.dma_start(proto_list[:], offs2)
-        nc.sync.dma_start(pf0[:], pf_rows[:, 0, :])
-        nc.sync.dma_start(pf1[:], pf_rows[:, 1, :])
-        nc.sync.dma_start(pf23[:], pf_rows[:, 2:4, :])
+        nc.sync.dma_start(pf1[:, 0:V], pf_rows[:, 1, :])
+        nc.sync.dma_start(pf23[:, 0 : 2 * V], pf_rows[:, 2:4, :].rearrange("p i v -> p (i v)"))
         load_scales(nc.scalar, wq_plane, wq_scales)
         nc.scalar.activation(warm_out[:], warm[:], TANH)
         load_scales(nc.scalar, pq_plane, pq_scales)
-        nc.scalar.dma_start(wq_codes[:].bitcast(I32), wq_words[0].bitcast(I32))
-        nc.scalar.dma_start(pq_codes[:].bitcast(I32), pq_words[0].bitcast(I32))
+        nc.sync.dma_start(wq_codes[:].bitcast(I32), wq_words[0].bitcast(I32))
+        nc.sync.dma_start(pq_codes[:].bitcast(I32), pq_words[0].bitcast(I32))
         for i in range(PACK):
             if i == 2:
                 nc.sync.dma_start(tok_list[:], offs)
@@ -73,16 +78,18 @@ def tile_list_remainder_on_prototype_kernel(tc, pq_words, pq_scales, wq_words, w
         nc.sync.dma_start(wf_codes[:].bitcast(I32), wf_words[0].rearrange("p n t -> p (n t)").bitcast(I32))
         load_scales(nc.sync, wf_plane, wf_scales)
 
-        def half_cols(h):
-            return slice(h * HALF, (h + 1) * HALF)
+        def entries(tile, j0, j1):
+            return tile[:, j0 // 16 : j1 // 16]
 
-        def list_half(tile, h):
-            return tile[:, h * LIST_COLS : (h + 1) * LIST_COLS]
-
-        picked = [sb.tile([P, PACK, HALF], F32, name="picked%d" % h, tag="stage%d" % h, align_bytes=64) for h in range(2)]
+        stage = sb.tile([P, 2048], F32, name="stage")
+        spare = sb.tile([P, 3, J], F32, name="spare")
+        picked = [spare[:, 0, :], spare[:, 1, :], spare[:, 2, :], stage[:, 1024:1536]]
+        d32 = [
+            stage[:, 0:1024].rearrange("p (i c) -> p i c", i=PACK),
+            stage[:].rearrange("p (i c) -> p i c", i=PACK)[:, :, 0:HALF],
+        ]
         for i in range(PACK):
-            for h in range(2):
-                nc.vector.tensor_copy(picked[h][:, i, :], pf_planes[i].indirect(list_half(proto_list, h)))
+            nc.vector.tensor_copy(picked[i], pf_planes[i].indirect(proto_list[:]))
 
         z_tiles = [sb.tile([P, V], F32, name="z%d" % m) for m in range(M_TILES)]
         for m in range(M_TILES):
@@ -98,58 +105,77 @@ def tile_list_remainder_on_prototype_kernel(tc, pq_words, pq_scales, wq_words, w
             )
             nc.scalar.copy(z_tiles[m][:], bank[:])
 
-        d32 = {}
         d16 = {}
-        d_codes = [sb.tile([P, HALF], U32, name="d_codes%d" % h, align_bytes=64) for h in range(2)]
-        d_plane = [sb.tile([P, HALF], U8, name="d_plane%d" % h, align_bytes=64) for h in range(2)]
-        act = [sb.tile([P, M_TILES, HALF], F32, name="act%d" % h) for h in range(2)]
-        res = [sb.tile([P, M_TILES, HALF], F32, name="res%d" % h) for h in range(2)]
+        d_codes = [sb.tile([P, j1 - j0], U32, name="d_codes%d" % j0, tag="codes%d" % j0, align_bytes=64) for j0, j1 in CHUNKS]
+        d_plane = [sb.tile([P, j1 - j0], U8, name="d_plane%d" % j0, align_bytes=64) for j0, j1 in CHUNKS]
+        act = {}
+        res = [sb.tile([P, M_TILES, j1 - j0], F32, name="res%d" % j0) for j0, j1 in CHUNKS]
         out_rows = out.rearrange("(m p) j -> p m j", p=P)
 
-        def remainder(h):
-            d32[h] = sb.tile([P, PACK, HALF], F32, name="d32_%d" % h, tag=("stage2", "stage0")[h], align_bytes=64)
-            for i in range(PACK):
-                nc.vector.tensor_tensor(d32[h][:, i, :], xf_planes[i][:].indirect(list_half(tok_list, h)), picked[h][:, i, :], SUB)
+        def remainder(c, i):
+            j0, j1 = CHUNKS[c]
+            proto = picked[i][:, j0:j1]
+            nc.vector.tensor_tensor(d32[c][:, i, :], xf_planes[i][:].indirect(entries(tok_list, j0, j1)), proto, SUB)
 
-        def weave(h, copy):
-            d16[h] = sb.tile([P, HALF, PACK], BF16, name="d16_%d" % h, tag=("stage3", "stage2")[h], align_bytes=64)
-            copy(d16[h][:].rearrange("p (c e) i -> p c i e", e=4), d32[h][:].rearrange("p i (c e) -> p c i e", e=4))
+        def weave(c, tag):
+            j0, j1 = CHUNKS[c]
+            d16[c] = sb.tile([P, j1 - j0, PACK], BF16, name="d16_%d" % c, tag=tag, align_bytes=64)
+            nc.scalar.copy(d16[c][:].rearrange("p (c e) i -> p c i e", e=4), d32[c].rearrange("p i (c e) -> p c i e", e=4))
 
-        def quantise(h):
-            nc.vector.quantize_mx(out=d_codes[h][:].bitcast(FP8X4), scales=d_plane[h][:], in_=d16[h][:].rearrange("p j i -> p (j i)"))
+        def quantise(c):
+            nc.vector.quantize_mx(out=d_codes[c][:].bitcast(FP8X4), scales=d_plane[c][:], in_=d16[c][:].rearrange("p j i -> p (j i)"))
 
-        def product(h):
-            for m in range(M_TILES):
-                bank = psum.tile([P, V], F32, name="bank")
-                nc.tensor.matmul_mx(
-                    out=bank[:, 0:HALF],
-                    lhsT=wf_codes[:, P * m : P * (m + 1)].bitcast(FP8X4),
-                    lhsT_scale=wf_plane[:, P * m : P * (m + 1)],
-                    rhs=d_codes[h][:].bitcast(FP8X4),
-                    rhs_scale=d_plane[h][:],
-                    start=True,
-                    stop=True,
-                )
-                nc.scalar.activation(act[h][:, m, :], bank[:, 0:HALF], TANH)
+        def product(c, m, dst):
+            nc.tensor.matmul_mx(
+                out=dst,
+                lhsT=wf_codes[:, P * m : P * (m + 1)].bitcast(FP8X4),
+                lhsT_scale=wf_plane[:, P * m : P * (m + 1)],
+                rhs=d_codes[c][:].bitcast(FP8X4),
+                rhs_scale=d_plane[c][:],
+                start=True,
+                stop=True,
+            )
 
-        def finish(h, m):
-            nc.vector.tensor_tensor(res[h][:, m, :], z_tiles[m][:].indirect(list_half(proto_list, h)), act[h][:, m, :], ADD)
+        def wide_product(c, m):
+            bank = psum.tile([P, V], F32, name="bank")
+            product(c, m, bank[:, 0:HALF])
+            return bank
 
-        def store(h, m0, m1):
-            nc.sync.dma_start(out_rows[:, m0:m1, half_cols(h)], res[h][:, m0:m1, :])
+        def wide_tanh(c, m, bank):
+            tile = sb.tile([P, HALF], F32, name="act%d_%d" % (c, m))
+            nc.scalar.activation(tile[:], bank[:, 0:HALF], TANH)
+            act[c, m] = tile[:]
 
-        remainder(0)
-        weave(0, nc.scalar.copy)
+        def finish(c, m):
+            j0, j1 = CHUNKS[c]
+            nc.vector.tensor_tensor(res[c][:, m, :], z_tiles[m][:].indirect(entries(proto_list, j0, j1)), act[c, m], ADD)
+
+        def store(c, m0, m1):
+            j0, j1 = CHUNKS[c]
+            nc.sync.dma_start(out_rows[:, m0:m1, j0:j1], res[c][:, m0:m1, :])
+
+        for i in range(PACK):
+            remainder(0, i)
+        weave(0, "d16_0")
+        remainder(1, 3)
+        remainder(1, 2)
         quantise(0)
-        product(0)
-        remainder(1)
-        weave(1, nc.vector.tensor_copy)
+        banks = [wide_product(0, m) for m in range(M_TILES)]
+        remainder(1, 0)
+        remainder(1, 1)
+        wide_tanh(0, 0, banks[0])
+        wide_tanh(0, 1, banks[1])
+        weave(1, "codes0")
+        wide_tanh(0, 2, banks[2])
+        wide_tanh(0, 3, banks[3])
         finish(0, 0)
+        finish(0, 1)
         quantise(1)
-        product(1)
-        for m in range(1, M_TILES):
-            finish(0, m)
+        finish(0, 2)
+        finish(0, 3)
         store(0, 0, 4)
+        for m in range(M_TILES):
+            wide_tanh(1, m, wide_product(1, m))
         for m in range(M_TILES):
             finish(1, m)
             if m > 0:

@@ -47,7 +47,7 @@ def tile_list_remainder_on_prototype_kernel(tc, pq_words, pq_scales, wq_words, w
         pf1 = sb.tile([P, WINDOW], F32, name="pf1")
         pf23 = sb.tile([P, V + WINDOW], F32, name="pf23")
         pf_planes = [pf0[:], pf1[:], pf23[:, 0:WINDOW], pf23[:, V:]]
-        xf_planes = [sb.tile([P, T], F32, name="xf%d" % i) for i in range(PACK)]
+        xf_planes = [sb.tile([P, T], F32, name="xf%d" % i, tag="xf%d" % i) for i in range(PACK)]
         wq_codes = sb.tile([P, 2 * N], U8, name="wq_codes", align_bytes=64)
         pq_codes = sb.tile([P, 2 * V], U8, name="pq_codes", align_bytes=64)
         wf_codes = sb.tile([P, N], U32, name="wf_codes", align_bytes=64)
@@ -81,17 +81,20 @@ def tile_list_remainder_on_prototype_kernel(tc, pq_words, pq_scales, wq_words, w
         def entries(tile, j0, j1):
             return tile[:, j0 // 16 : j1 // 16]
 
-        stage = sb.tile([P, 2048], F32, name="stage")
+        stage = sb.tile([P, 6, J], F32, name="stage")
         spare = sb.tile([P, 3, J], F32, name="spare")
-        picked = [spare[:, 0, :], spare[:, 1, :], spare[:, 2, :], stage[:, 1024:1536]]
-        d32 = [
-            stage[:, 0:1024].rearrange("p (i c) -> p i c", i=PACK),
-            stage[:].rearrange("p (i c) -> p i c", i=PACK)[:, :, 0:HALF],
-        ]
+        picked = [spare[:, 0, :], spare[:, 1, :], spare[:, 2, :], stage[:, 4, :]]
+        d32 = [stage[:, 0:4, 0:HALF], stage[:, 2:6, 0:HALF]]
         for i in range(PACK):
             nc.vector.tensor_copy(picked[i], pf_planes[i].indirect(proto_list[:]))
 
-        z_tiles = [sb.tile([P, V], F32, name="z%d" % m) for m in range(M_TILES)]
+        z_tiles = {}
+        z_banks = []
+
+        def keep_z(m, tag):
+            z_tiles[m] = sb.tile([P, V], F32, name="z%d" % m, tag=tag)
+            nc.scalar.copy(z_tiles[m][:], z_banks[m][:])
+
         for m in range(M_TILES):
             bank = psum.tile([P, V], F32, name="bank")
             nc.tensor.matmul_mx(
@@ -103,7 +106,9 @@ def tile_list_remainder_on_prototype_kernel(tc, pq_words, pq_scales, wq_words, w
                 start=True,
                 stop=True,
             )
-            nc.scalar.copy(z_tiles[m][:], bank[:])
+            z_banks.append(bank)
+            if m < 2:
+                keep_z(m, "z%d" % m)
 
         d16 = {}
         d_codes = [sb.tile([P, j1 - j0], U32, name="d_codes%d" % j0, tag="codes%d" % j0, align_bytes=64) for j0, j1 in CHUNKS]
@@ -117,10 +122,8 @@ def tile_list_remainder_on_prototype_kernel(tc, pq_words, pq_scales, wq_words, w
             proto = picked[i][:, j0:j1]
             nc.vector.tensor_tensor(d32[c][:, i, :], xf_planes[i][:].indirect(entries(tok_list, j0, j1)), proto, SUB)
 
-        def weave(c, tag):
-            j0, j1 = CHUNKS[c]
-            d16[c] = sb.tile([P, j1 - j0, PACK], BF16, name="d16_%d" % c, tag=tag, align_bytes=64)
-            nc.scalar.copy(d16[c][:].rearrange("p (c e) i -> p c i e", e=4), d32[c].rearrange("p i (c e) -> p c i e", e=4))
+        def weave(c, i0, i1):
+            nc.scalar.copy(d16[c][:, :, i0:i1].rearrange("p (c e) i -> p c i e", e=4), d32[c][:, i0:i1, :].rearrange("p i (c e) -> p c i e", e=4))
 
         def quantise(c):
             nc.vector.quantize_mx(out=d_codes[c][:].bitcast(FP8X4), scales=d_plane[c][:], in_=d16[c][:].rearrange("p j i -> p (j i)"))
@@ -154,18 +157,23 @@ def tile_list_remainder_on_prototype_kernel(tc, pq_words, pq_scales, wq_words, w
             j0, j1 = CHUNKS[c]
             nc.sync.dma_start(out_rows[:, m0:m1, j0:j1], res[c][:, m0:m1, :])
 
+        d16[0] = sb.tile([P, HALF, PACK], BF16, name="d16_0", align_bytes=64)
         for i in range(PACK):
             remainder(0, i)
-        weave(0, "d16_0")
+            if i % 2 == 1:
+                weave(0, i - 1, i + 1)
         remainder(1, 3)
+        keep_z(3, "xf3")
         remainder(1, 2)
+        keep_z(2, "xf2")
         quantise(0)
         banks = [wide_product(0, m) for m in range(M_TILES)]
         remainder(1, 0)
         remainder(1, 1)
         wide_tanh(0, 0, banks[0])
         wide_tanh(0, 1, banks[1])
-        weave(1, "codes0")
+        d16[1] = sb.tile([P, HALF, PACK], BF16, name="d16_1", tag="codes0", align_bytes=64)
+        weave(1, 0, PACK)
         wide_tanh(0, 2, banks[2])
         wide_tanh(0, 3, banks[3])
         finish(0, 0)

from contextlib import ExitStack

import concourse.mybir as mybir

K, V, T, J, N = 512, 512, 1024, 512, 512
FLOPS = 2 * K * N * V + 2 * K * N * J

F32 = mybir.dt.float32
BF16 = mybir.dt.bfloat16
I32 = mybir.dt.int32
U32 = mybir.dt.uint32
U16 = mybir.dt.uint16
U8 = mybir.dt.uint8
FP8X4 = mybir.dt.float8_e4m3fn_x4
FP4X4 = mybir.dt.float4_e2m1fn_x4
ADD = mybir.AluOpType.add
SUB = mybir.AluOpType.subtract
TANH = mybir.ActivationFunctionType.Tanh

P = 128
PACK = 4
HALF = J // 2
LIST_COLS = HALF // 16
M_TILES = N // P
CHUNKS = ((0, 256), (256, 512))
WINDOW = 704


def load_scales(queue, plane, scales):
    for q in range(4):
        queue.dma_start(plane[32 * q : 32 * q + 4, :].bitcast(I32), scales[0, 4 * q : 4 * q + 4, :].bitcast(I32))


def tile_list_remainder_on_prototype_kernel(tc, pq_words, pq_scales, wq_words, wq_scales, xf, pf, wf_words, wf_scales, offs, offs2, out):
    nc = tc.nc
    with ExitStack() as ctx:
        lists = ctx.enter_context(tc.tile_pool(name="lists", bufs=1))
        sb = ctx.enter_context(tc.tile_pool(name="sb", bufs=1))
        psum = ctx.enter_context(tc.psum_pool(name="psum", bufs=8))

        tok_list = lists.tile([P, J // 16], U16, name="tok_list")
        proto_list = lists.tile([P, J // 16], U16, name="proto_list")
        pf_rows = pf.rearrange("(p i) v -> p i v", i=PACK)
        xf_rows = xf.rearrange("(p i) t -> p i t", i=PACK)

        pf0 = sb.tile([P, WINDOW], F32, name="pf0")
        pf1 = sb.tile([P, WINDOW], F32, name="pf1")
        pf23 = sb.tile([P, V + WINDOW], F32, name="pf23")
        pf_planes = [pf0[:], pf1[:], pf23[:, 0:WINDOW], pf23[:, V:]]
        xf_planes = [sb.tile([P, T], F32, name="xf%d" % i, tag="xf%d" % i) for i in range(PACK)]
        wq_codes = sb.tile([P, 2 * N], U8, name="wq_codes", align_bytes=64)
        pq_codes = sb.tile([P, 2 * V], U8, name="pq_codes", align_bytes=64)
        wf_codes = sb.tile([P, N], U32, name="wf_codes", align_bytes=64)
        wq_plane = sb.tile([P, N], U8, name="wq_plane", align_bytes=64)
        pq_plane = sb.tile([P, V], U8, name="pq_plane", align_bytes=64)
        wf_plane = sb.tile([P, N], U8, name="wf_plane", align_bytes=64)

        warm = sb.tile([P, 8], F32, name="warm")
        warm_out = sb.tile([P, 8], F32, name="warm_out")
        nc.vector.memset(warm[:], 0.0)
        nc.vector.memset(pf0[:, V:], 0.0)
        nc.vector.memset(pf1[:, V:], 0.0)
        nc.vector.memset(pf23[:, 2 * V :], 0.0)

        nc.sync.dma_start(pf0[:, 0:V], pf_rows[:, 0, :])
        nc.sync.dma_start(proto_list[:], offs2)
        nc.sync.dma_start(pf1[:, 0:V], pf_rows[:, 1, :])
        nc.sync.dma_start(pf23[:, 0 : 2 * V], pf_rows[:, 2:4, :].rearrange("p i v -> p (i v)"))
        load_scales(nc.scalar, wq_plane, wq_scales)
        nc.scalar.activation(warm_out[:], warm[:], TANH)
        load_scales(nc.scalar, pq_plane, pq_scales)
        nc.sync.dma_start(wq_codes[:].bitcast(I32), wq_words[0].bitcast(I32))
        nc.sync.dma_start(pq_codes[:].bitcast(I32), pq_words[0].bitcast(I32))
        for i in range(PACK):
            if i == 2:
                nc.sync.dma_start(tok_list[:], offs)
            nc.sync.dma_start(xf_planes[i][:], xf_rows[:, i, :])
        nc.sync.dma_start(wf_codes[:].bitcast(I32), wf_words[0].rearrange("p n t -> p (n t)").bitcast(I32))
        load_scales(nc.sync, wf_plane, wf_scales)

        def entries(tile, j0, j1):
            return tile[:, j0 // 16 : j1 // 16]

        stage = sb.tile([P, 6, J], F32, name="stage")
        spare = sb.tile([P, 3, J], F32, name="spare")
        picked = [spare[:, 0, :], spare[:, 1, :], spare[:, 2, :], stage[:, 4, :]]
        d32 = [stage[:, 0:4, 0:HALF], stage[:, 2:6, 0:HALF]]
        for i in range(PACK):
            nc.vector.tensor_copy(picked[i], pf_planes[i].indirect(proto_list[:]))

        z_tiles = {}
        z_banks = []

        def keep_z(m, tag):
            z_tiles[m] = sb.tile([P, V], F32, name="z%d" % m, tag=tag)
            nc.scalar.copy(z_tiles[m][:], z_banks[m][:])

        for m in range(M_TILES):
            bank = psum.tile([P, V], F32, name="bank")
            nc.tensor.matmul_mx(
                out=bank[:],
                lhsT=wq_codes[:, 2 * P * m : 2 * P * (m + 1)].bitcast(FP4X4),
                lhsT_scale=wq_plane[:, P * m : P * (m + 1)],
                rhs=pq_codes[:].bitcast(FP4X4),
                rhs_scale=pq_plane[:],
                start=True,
                stop=True,
            )
            z_banks.append(bank)
            if m < 2:
                keep_z(m, "z%d" % m)

        d16 = {}
        d_codes = [sb.tile([P, j1 - j0], U32, name="d_codes%d" % j0, tag="codes%d" % j0, align_bytes=64) for j0, j1 in CHUNKS]
        d_plane = [sb.tile([P, j1 - j0], U8, name="d_plane%d" % j0, align_bytes=64) for j0, j1 in CHUNKS]
        act = {}
        res = [sb.tile([P, M_TILES, j1 - j0], F32, name="res%d" % j0) for j0, j1 in CHUNKS]
        out_rows = out.rearrange("(m p) j -> p m j", p=P)

        def remainder(c, i):
            j0, j1 = CHUNKS[c]
            proto = picked[i][:, j0:j1]
            nc.vector.tensor_tensor(d32[c][:, i, :], xf_planes[i][:].indirect(entries(tok_list, j0, j1)), proto, SUB)

        def weave(c, i0, i1):
            nc.scalar.copy(d16[c][:, :, i0:i1].rearrange("p (c e) i -> p c i e", e=4), d32[c][:, i0:i1, :].rearrange("p i (c e) -> p c i e", e=4))

        def quantise(c):
            nc.vector.quantize_mx(out=d_codes[c][:].bitcast(FP8X4), scales=d_plane[c][:], in_=d16[c][:].rearrange("p j i -> p (j i)"))

        def product(c, m, dst):
            nc.tensor.matmul_mx(
                out=dst,
                lhsT=wf_codes[:, P * m : P * (m + 1)].bitcast(FP8X4),
                lhsT_scale=wf_plane[:, P * m : P * (m + 1)],
                rhs=d_codes[c][:].bitcast(FP8X4),
                rhs_scale=d_plane[c][:],
                start=True,
                stop=True,
            )

        def wide_product(c, m):
            bank = psum.tile([P, V], F32, name="bank")
            product(c, m, bank[:, 0:HALF])
            return bank

        def wide_tanh(c, m, bank):
            tile = sb.tile([P, HALF], F32, name="act%d_%d" % (c, m))
            nc.scalar.activation(tile[:], bank[:, 0:HALF], TANH)
            act[c, m] = tile[:]

        def finish(c, m):
            j0, j1 = CHUNKS[c]
            nc.vector.tensor_tensor(res[c][:, m, :], z_tiles[m][:].indirect(entries(proto_list, j0, j1)), act[c, m], ADD)

        def store(c, m0, m1):
            j0, j1 = CHUNKS[c]
            nc.sync.dma_start(out_rows[:, m0:m1, j0:j1], res[c][:, m0:m1, :])

        d16[0] = sb.tile([P, HALF, PACK], BF16, name="d16_0", align_bytes=64)
        for i in range(PACK):
            remainder(0, i)
            if i % 2 == 1:
                weave(0, i - 1, i + 1)
        remainder(1, 3)
        keep_z(3, "xf3")
        remainder(1, 2)
        keep_z(2, "xf2")
        quantise(0)
        banks = [wide_product(0, m) for m in range(M_TILES)]
        remainder(1, 0)
        remainder(1, 1)
        wide_tanh(0, 0, banks[0])
        wide_tanh(0, 1, banks[1])
        d16[1] = sb.tile([P, HALF, PACK], BF16, name="d16_1", tag="codes0", align_bytes=64)
        weave(1, 0, PACK)
        wide_tanh(0, 2, banks[2])
        wide_tanh(0, 3, banks[3])
        finish(0, 0)
        finish(0, 1)
        quantise(1)
        finish(0, 2)
        finish(0, 3)
        store(0, 0, 4)
        for m in range(M_TILES):
            wide_tanh(1, m, wide_product(1, m))
        for m in range(M_TILES):
            finish(1, m)
            if m > 0:
                store(1, 0 if m == 1 else m, m + 1)
